import numpy as np
import ml_dtypes


def mxq(x, axis, fmt="e4m3"):
    dtype, down = {"e4m3": (ml_dtypes.float8_e4m3fn, 7), "e5m2": (ml_dtypes.float8_e5m2, 14)}[fmt]
    v = np.moveaxis(np.asarray(x, np.float32).astype(ml_dtypes.bfloat16).astype(np.float64), axis, -1)
    blocks = v.reshape(v.shape[:-1] + (-1, 32))
    amax = np.abs(blocks).max(-1, keepdims=True)
    byte = np.maximum(np.where(amax > 0, np.frexp(amax)[1] - 1 + 127, 0) - down, 1)
    scale = np.exp2(byte - 127.0)
    codes = (blocks / scale).astype(np.float32).astype(dtype).astype(np.float64)
    return np.moveaxis((codes * scale).reshape(v.shape), -1, axis)


WIDE = False


def mx_kscale(k):
    if not WIDE:
        return np.ones(k)
    levels = np.array([10, -10, 5, -5, 0])
    if k % 512:
        return np.exp2(np.random.permutation(np.resize(levels, k // 32))).repeat(32)
    a = np.empty((k // 512, 16))
    for p in range(k // 512):
        a[p, :8] = np.random.permutation(np.resize(levels, 8))
        for g in range(8):
            far = levels[np.abs(levels - a[p, g]) >= 10]
            a[p, g + 8] = far[np.random.randint(len(far))]
    return np.exp2(a.ravel()).repeat(32)


def f64(x):
    return np.asarray(x).astype(np.float64)


def striped(idx):
    return np.tile(idx.reshape(-1, 16).T, (8, 1)).astype(np.uint16)


def unstriped(offs):
    return offs[:16].T.reshape(-1).astype(np.int64)


E2M1 = np.array([0.0, 0.5, 1.0, 1.5, 2.0, 3.0, 4.0, 6.0, -0.0, -0.5, -1.0, -1.5, -2.0, -3.0, -4.0, -6.0])


def pack_fp4(w):
    k, n = w.shape
    w = f64(np.asarray(w, np.float32).astype(ml_dtypes.bfloat16)).reshape(k // 32, 32, n)
    amax = np.abs(w).max(1)
    mant, ex = np.frexp(amax / 6.0)
    byte = np.clip(np.where(amax > 0, np.where(mant > 0.5, ex, ex - 1) + 127, 1), 1, 254)
    scaled = (w * np.exp2(127.0 - byte)[:, None, :]).reshape(k, n).astype(np.float32)
    c = np.ascontiguousarray(scaled.reshape(k // 512, 128, 4, n).transpose(0, 1, 3, 2)).astype(ml_dtypes.float4_e2m1fn).view(np.uint8) & 0xF
    words = (c[..., 0::2] | (c[..., 1::2] << 4)).reshape(k // 512, 128, 2 * n)
    return np.ascontiguousarray(words), np.ascontiguousarray(byte.astype(np.uint8).reshape(k // 512, 16, n))


def unpack_fp4(words, scales):
    g, _, n = scales.shape
    words = np.ascontiguousarray(words).reshape(g, 128, n, 2)
    nib = np.empty((g, 128, n, 4), np.uint8)
    nib[..., 0::2] = words & 0xF
    nib[..., 1::2] = words >> 4
    vals = E2M1[nib] * np.repeat(np.exp2(scales.astype(np.float64) - 127.0), 8, axis=1)[..., None]
    return vals.transpose(0, 1, 3, 2).reshape(g * 512, n)


def gelu(v):
    return 0.5 * v * (1.0 + np.tanh(np.sqrt(2.0 / np.pi) * (v + 0.044715 * v**3)))

def planes(y):
    n, m = y.shape
    v = y.astype(np.float32).astype(ml_dtypes.bfloat16).astype(np.float64).reshape(n // 32, 32, m)
    top = np.abs(v).max(1)
    byte = np.clip(np.where(top > 0, np.frexp(top)[1] - 1 + 127 - 7, 1), 1, 254)
    codes = (v * np.exp2(127.0 - byte)[:, None, :]).reshape(n, m).astype(np.float32).astype(ml_dtypes.float8_e4m3fn).view(np.uint8)
    words = codes.reshape(n // 512, 128, 4, m).transpose(0, 1, 3, 2)
    return np.ascontiguousarray(words), np.ascontiguousarray(byte.astype(np.uint8).reshape(n // 512, 16, m))


K, T, N = 1024, 1024, 512
P = 2 ** 7


def setup_inputs():
    n = np.random.standard_normal
    s = mx_kscale(K)[:, None]
    packed_xT = pack_fp4(n((K, T)) * s)
    return {
        "x_words": packed_xT[0],
        "x_scales": packed_xT[1],
        "w1": (n((K, N)) / np.sqrt(K) / s).astype(np.float32),
        "frac": np.tile(np.random.uniform(0.05, 0.95, T), (P, 1)).astype(np.float32),
        "left": striped(np.random.permutation(T)),
        "right": striped(np.random.permutation(T)),
    }


def reference(x_words, x_scales, w1, frac, left, right):
    xq = unpack_fp4(x_words, x_scales)
    y = gelu(mxq(f64(w1), 0, "e4m3").T @ xq)
    l = y[:, unstriped(left)]
    out_0 = l + (y[:, unstriped(right)] - l) * f64(frac)[:1]
    return (out_0,) + planes(out_0)

@@ -1,0 +1,227 @@
+from contextlib import ExitStack
+
+import concourse.mybir as mybir
+from concourse.masks import make_identity
+
+K, T, N = 1024, 1024, 512
+FLOPS = 2 * K * T * N
+
+F32 = mybir.dt.float32
+BF16 = mybir.dt.bfloat16
+I32 = mybir.dt.int32
+U32 = mybir.dt.uint32
+U16 = mybir.dt.uint16
+U8 = mybir.dt.uint8
+FP8X4 = mybir.dt.float8_e4m3fn_x4
+FP4X4 = mybir.dt.float4_e2m1fn_x4
+ALU = mybir.AluOpType
+ACT = mybir.ActivationFunctionType
+
+P = 128
+PACK = 4
+PASSES = K // (P * PACK)
+BANK = 512
+BLOCKS = N // P
+W_COLS = 256
+CHUNKS = (256, 256, 256, 128, 128)
+
+
+def tile_picked_wlerp_gelu_lo_kernel(tc, x_words, x_scales, w1, frac, left, right, out_0, out_1, out_2):
+    nc = tc.nc
+    with ExitStack() as ctx:
+        keep = ctx.enter_context(tc.tile_pool(name="keep", bufs=1))
+        ring = ctx.enter_context(tc.tile_pool(name="ring", bufs=4))
+        psum = ctx.enter_context(tc.psum_pool(name="psum", bufs=6))
+
+        left_sb = keep.tile([P, T // 16], U16, name="left_sb")
+        right_sb = keep.tile([P, T // 16], U16, name="right_sb")
+
+        xs = keep.tile([P, PASSES, T], U8, name="xs", align_bytes=64)
+        nc.gpsimd.memset(xs[:].rearrange("p g c -> p (g c)").bitcast(I32), 0)
+        warm_in = keep.tile([P, 1], F32, name="warm_in")
+        warm_out = keep.tile([P, 1], F32, name="warm_out")
+        nc.gpsimd.memset(warm_in[:], 0.0)
+        nc.scalar.activation(out=warm_out[:], in_=warm_in[:], func=ACT.Gelu_apprx_tanh)
+
+        ident = keep.tile([P, P], F32, name="ident")
+        make_identity(nc, ident[:])
+
+        raw = {}
+        xw = {}
+
+        def load_w(a, g):
+            tag = "raw%d" % g if a == 0 else "left%d" % g
+            raw[a, g] = keep.tile([P, PACK, W_COLS], F32, name="raw%d%d" % (a, g), tag=tag)
+            rows = w1[g * P * PACK : (g + 1) * P * PACK, a * W_COLS : (a + 1) * W_COLS]
+            nc.sync.dma_start(out=raw[a, g][:], in_=rows.rearrange("(p j) c -> p j c", j=PACK))
+
+        def load_x(g):
+            xw[g] = keep.tile([P, 2 * T], U8, name="xw%d" % g, align_bytes=64)
+            nc.sync.dma_start(out=xw[g][:].bitcast(I32), in_=x_words[g].bitcast(I32))
+
+        first = CHUNKS[0]
+        f_head = keep.tile([P, first], F32, name="f_head")
+        g_head = keep.tile([P, first], F32, name="g_head")
+        f_rest = keep.tile([P, T - first], F32, name="f_rest")
+        g_rest = keep.tile([P, T - first], F32, name="g_rest")
+
+        load_w(0, 0)
+        load_x(0)
+        for q in range(4):
+            nc.sync.dma_start(
+                out=xs[32 * q : 32 * q + 4, :, :].bitcast(I32),
+                in_=x_scales[:, 4 * q : 4 * q + 4, :].rearrange("g r c -> r g c").bitcast(I32),
+            )
+        load_w(0, 1)
+        load_x(1)
+        nc.sync.dma_start(left_sb[:], left)
+        nc.sync.dma_start(right_sb[:], right)
+        nc.sync.dma_start(out=f_head[:], in_=frac[:, 0:first])
+        load_w(1, 0)
+        load_w(1, 1)
+        nc.sync.dma_start(out=f_rest[:], in_=frac[:, first:T])
+
+        w_codes = {}
+        w_scales = {}
+
+        def quantize_w(a, g, c0, width):
+            label = "%d%d_%d" % (a, g, c0)
+            grouped = keep.tile([P, width, PACK], BF16, name="wg" + label, align_bytes=64)
+            nc.vector.tensor_copy(
+                out=grouped[:].rearrange("p (c i) j -> p c j i", i=4),
+                in_=raw[a, g][:, :, c0 : c0 + width].rearrange("p j (c i) -> p c j i", i=4),
+            )
+            tag = "right1" if label == "11_0" else "wc" + label
+            wc = keep.tile([P, width], U32, name="wc" + label, tag=tag, align_bytes=64)
+            ws = keep.tile([P, width], U8, name="ws" + label, align_bytes=64)
+            nc.vector.quantize_mx(
+                out=wc[:].bitcast(FP8X4),
+                scales=ws[:],
+                in_=grouped[:].rearrange("p c j -> p (c j)"),
+            )
+            for i in range(width // P):
+                b = 2 * a + c0 // P + i
+                w_codes[b, g] = wc[:, i * P : (i + 1) * P]
+                w_scales[b, g] = ws[:, i * P : (i + 1) * P]
+
+        y = [keep.tile([P, T], F32, name="y%d" % b) for b in range(BLOCKS)]
+
+        def project(a):
+            blocks = (2 * a, 2 * a + 1)
+            acc = {}
+            for b in blocks:
+                for h in range(T // BANK):
+                    acc[b, h] = psum.tile([P, BANK], F32, name="acc%d%d" % (b, h), tag="bank")
+
+            def one_pass(b, h, g):
+                nc.tensor.matmul_mx(
+                    out=acc[b, h][:],
+                    lhsT=w_codes[b, g].bitcast(FP8X4),
+                    lhsT_scale=w_scales[b, g],
+                    rhs=xw[g][:, 2 * h * BANK : 2 * (h + 1) * BANK].bitcast(FP4X4),
+                    rhs_scale=xs[:, g, h * BANK : (h + 1) * BANK],
+                    start=(g == 0),
+                    stop=(g == PASSES - 1),
+                )
+
+            quantize_w(a, 0, 0, W_COLS)
+            for b in blocks:
+                quantize_w(a, 1, (b % 2) * P, P)
+                for g in range(PASSES):
+                    for h in range(T // BANK):
+                        one_pass(b, h, g)
+                        if g == PASSES - 1:
+                            nc.scalar.activation(
+                                out=y[b][:, h * BANK : (h + 1) * BANK],
+                                in_=acc[b, h][:],
+                                func=ACT.Gelu_apprx_tanh,
+                            )
+
+        project(0)
+        nc.vector.tensor_scalar(
+            out=g_head[:], in0=f_head[:], scalar1=-1.0, scalar2=1.0, op0=ALU.mult, op1=ALU.add
+        )
+        project(1)
+        nc.scalar.activation(out=g_rest[:], in_=f_rest[:], func=ACT.Copy, scale=-1.0, bias=1.0)
+
+        codes = keep.tile([P, T], U32, name="codes", align_bytes=64)
+        scales = keep.tile([P, T], U8, name="scales", align_bytes=64)
+        out_rows = out_0.rearrange("(l t) v -> l t v", t=PACK)
+        out_words = out_1[0].rearrange("l v t -> l (v t)").bitcast(I32)
+
+        def front(v0, width, between):
+            if v0 == 0:
+                f_part, g_part = f_head[:], g_head[:]
+            else:
+                f_part = f_rest[:, v0 - first : v0 - first + width]
+                g_part = g_rest[:, v0 - first : v0 - first + width]
+            offs = slice(v0 // 16, (v0 + width) // 16)
+            turned = [psum.tile([P, BLOCKS, P], F32, name="turned", bufs=2) for s in range(width // P)]
+            for b in range(BLOCKS):
+                from_left = keep.tile([P, width], F32, name="from_left", tag="left%d" % (b % 2))
+                from_right = keep.tile([P, width], F32, name="from_right", tag="right%d" % (b % 2), align_bytes=64)
+                nc.vector.tensor_tensor(from_left[:], y[b][:].indirect(left_sb[:, offs]), g_part, ALU.mult)
+                nc.vector.tensor_tensor(from_right[:], y[b][:].indirect(right_sb[:, offs]), f_part, ALU.mult)
+                for s in range(width // P):
+                    cols = slice(s * P, (s + 1) * P)
+                    nc.tensor.matmul(turned[s][:, b, :], from_left[:, cols], ident[:], start=True, stop=False, is_transpose=True)
+                    nc.tensor.matmul(turned[s][:, b, :], from_right[:, cols], ident[:], start=False, stop=True, is_transpose=True)
+                if b == 0:
+                    between()
+            dealt = []
+            for s in range(width // P):
+                tile = ring.tile([P, PACK, P], F32, name="dealt")
+                nc.scalar.copy(
+                    out=tile[:].rearrange("p t (b l) -> p t b l", b=BLOCKS),
+                    in_=turned[s][:].rearrange("p b (l t) -> p t b l", t=PACK),
+                )
+                dealt.append(tile)
+            return dealt
+
+        def back(v0, width, dealt, last):
+            result = ring.tile([P, PACK, width], F32, name="result")
+            rounded = ring.tile([P, width, PACK], BF16, name="rounded", align_bytes=64)
+            for s in range(width // P):
+                cols = slice(s * P, (s + 1) * P)
+                bank = psum.tile([P, PACK, P], F32, name="upright", tag="bank")
+                for t in range(PACK):
+                    nc.tensor.transpose(bank[:, t, :], dealt[s][:, t, :], ident[:])
+                if last:
+                    nc.vector.tensor_copy(out=rounded[:, cols, :], in_=bank[:].rearrange("p t v -> p v t"))
+                    nc.scalar.copy(out=result[:, :, cols], in_=bank[:])
+                else:
+                    nc.scalar.copy(out=result[:, :, cols], in_=bank[:])
+                    nc.scalar.copy(out=rounded[:, cols, :], in_=bank[:].rearrange("p t v -> p v t"))
+            nc.sync.dma_start(out=out_rows[:, :, v0 : v0 + width], in_=result[:])
+            return rounded
+
+        def planes(v0, width, rounded):
+            nc.vector.quantize_mx(
+                out=codes[:, v0 : v0 + width].bitcast(FP8X4),
+                scales=scales[:, v0 : v0 + width],
+                in_=rounded[:].rearrange("p v t -> p (v t)"),
+            )
+            nc.sync.dma_start(out=out_words[:, v0 : v0 + width], in_=codes[:, v0 : v0 + width].bitcast(I32))
+
+        starts = [sum(CHUNKS[:c]) for c in range(len(CHUNKS))]
+        dealt_of = {}
+        rounded_of = {}
+
+        def finish(c):
+            if c >= 0:
+                rounded_of[c] = back(starts[c], CHUNKS[c], dealt_of[c], c == len(CHUNKS) - 1)
+
+        for c in range(len(CHUNKS)):
+            dealt_of[c] = front(starts[c], CHUNKS[c], lambda: finish(c - 1))
+            if c >= 1:
+                planes(starts[c - 1], CHUNKS[c - 1], rounded_of[c - 1])
+        last = len(CHUNKS) - 1
+        finish(last)
+        planes(starts[last], CHUNKS[last], rounded_of[last])
+
+        for q in range(4):
+            queue = nc.sync if q % 2 == 0 else nc.scalar
+            queue.dma_start(
+                out=out_2[0, 4 * q : 4 * q + 4, :].bitcast(I32),
+                in_=scales[32 * q : 32 * q + 4, :].bitcast(I32),
+            )

@@ -22,8 +22,8 @@ PACK = 4
 PASSES = K // (P * PACK)
 BANK = 512
 BLOCKS = N // P
-W_COLS = 256
-CHUNKS = (256, 256, 256, 128, 128)
+CHUNKS = (384, 256, 256, 128)
+QUANT = (512, 256, 128, 128)
 
 
 def tile_picked_wlerp_gelu_lo_kernel(tc, x_words, x_scales, w1, frac, left, right, out_0, out_1, out_2):
@@ -31,7 +31,7 @@ def tile_picked_wlerp_gelu_lo_kernel(tc, x_words, x_scales, w1, frac, left, righ
     with ExitStack() as ctx:
         keep = ctx.enter_context(tc.tile_pool(name="keep", bufs=1))
         ring = ctx.enter_context(tc.tile_pool(name="ring", bufs=4))
-        psum = ctx.enter_context(tc.psum_pool(name="psum", bufs=6))
+        psum = ctx.enter_context(tc.psum_pool(name="psum", bufs=5))
 
         left_sb = keep.tile([P, T // 16], U16, name="left_sb")
         right_sb = keep.tile([P, T // 16], U16, name="right_sb")
@@ -49,11 +49,13 @@ def tile_picked_wlerp_gelu_lo_kernel(tc, x_words, x_scales, w1, frac, left, righ
         raw = {}
         xw = {}
 
-        def load_w(a, g):
-            tag = "raw%d" % g if a == 0 else "left%d" % g
-            raw[a, g] = keep.tile([P, PACK, W_COLS], F32, name="raw%d%d" % (a, g), tag=tag)
-            rows = w1[g * P * PACK : (g + 1) * P * PACK, a * W_COLS : (a + 1) * W_COLS]
-            nc.sync.dma_start(out=raw[a, g][:], in_=rows.rearrange("(p j) c -> p j c", j=PACK))
+        def load_w(b, g, blocks):
+            label = "raw%d%d" % (b, g)
+            tile = keep.tile([P, PACK, blocks * P], F32, name=label)
+            rows = w1[g * P * PACK : (g + 1) * P * PACK, b * P : (b + blocks) * P]
+            nc.sync.dma_start(out=tile[:], in_=rows.rearrange("(p j) c -> p j c", j=PACK))
+            for i in range(blocks):
+                raw[b + i, g] = tile[:, :, i * P : (i + 1) * P]
 
         def load_x(g):
             xw[g] = keep.tile([P, 2 * T], U8, name="xw%d" % g, align_bytes=64)
@@ -65,44 +67,49 @@ def tile_picked_wlerp_gelu_lo_kernel(tc, x_words, x_scales, w1, frac, left, righ
         f_rest = keep.tile([P, T - first], F32, name="f_rest")
         g_rest = keep.tile([P, T - first], F32, name="g_rest")
 
-        load_w(0, 0)
+        load_w(0, 0, 2)
         load_x(0)
         for q in range(4):
             nc.sync.dma_start(
                 out=xs[32 * q : 32 * q + 4, :, :].bitcast(I32),
                 in_=x_scales[:, 4 * q : 4 * q + 4, :].rearrange("g r c -> r g c").bitcast(I32),
             )
-        load_w(0, 1)
+        load_w(0, 1, 2)
         load_x(1)
+        nc.sync.dma_start(out=f_head[:], in_=frac[:, 0:first])
         nc.sync.dma_start(left_sb[:], left)
         nc.sync.dma_start(right_sb[:], right)
-        nc.sync.dma_start(out=f_head[:], in_=frac[:, 0:first])
-        load_w(1, 0)
-        load_w(1, 1)
+        for b in (2, 3):
+            for g in range(PASSES):
+                load_w(b, g, 1)
         nc.sync.dma_start(out=f_rest[:], in_=frac[:, first:T])
 
         w_codes = {}
         w_scales = {}
 
-        def quantize_w(a, g, c0, width):
-            label = "%d%d_%d" % (a, g, c0)
-            grouped = keep.tile([P, width, PACK], BF16, name="wg" + label, align_bytes=64)
-            nc.vector.tensor_copy(
-                out=grouped[:].rearrange("p (c i) j -> p c j i", i=4),
-                in_=raw[a, g][:, :, c0 : c0 + width].rearrange("p j (c i) -> p c j i", i=4),
+        grouped_tag = {(0, 1): "hold", (2, 0): "left0", (2, 1): "right0", (3, 0): "right1", (3, 1): "left1"}
+        codes_tag = {(1, 0): "hold"}
+
+        def quantize_w(b, g):
+            label = "%d%d" % (b, g)
+            grouped = keep.tile(
+                [P, P, PACK], BF16, name="wg" + label, tag=grouped_tag.get((b, g), "wg" + label), align_bytes=64
             )
-            tag = "right1" if label == "11_0" else "wc" + label
-            wc = keep.tile([P, width], U32, name="wc" + label, tag=tag, align_bytes=64)
-            ws = keep.tile([P, width], U8, name="ws" + label, align_bytes=64)
+            dst = grouped[:].rearrange("p (c i) j -> p c j i", i=4)
+            src = raw[b, g].rearrange("p j (c i) -> p c j i", i=4)
+            if (b, g) == (3, 0):
+                nc.scalar.copy(out=dst, in_=src)
+            else:
+                nc.vector.tensor_copy(out=dst, in_=src)
+            wc = keep.tile([P, P], U32, name="wc" + label, tag=codes_tag.get((b, g), "wc" + label), align_bytes=64)
+            ws = keep.tile([P, P], U8, name="ws" + label, align_bytes=64)
             nc.vector.quantize_mx(
                 out=wc[:].bitcast(FP8X4),
                 scales=ws[:],
                 in_=grouped[:].rearrange("p c j -> p (c j)"),
             )
-            for i in range(width // P):
-                b = 2 * a + c0 // P + i
-                w_codes[b, g] = wc[:, i * P : (i + 1) * P]
-                w_scales[b, g] = ws[:, i * P : (i + 1) * P]
+            w_codes[b, g] = wc[:]
+            w_scales[b, g] = ws[:]
 
         y = [keep.tile([P, T], F32, name="y%d" % b) for b in range(BLOCKS)]
 
@@ -124,9 +131,9 @@ def tile_picked_wlerp_gelu_lo_kernel(tc, x_words, x_scales, w1, frac, left, righ
                     stop=(g == PASSES - 1),
                 )
 
-            quantize_w(a, 0, 0, W_COLS)
             for b in blocks:
-                quantize_w(a, 1, (b % 2) * P, P)
+                quantize_w(b, 0)
+                quantize_w(b, 1)
                 for g in range(PASSES):
                     for h in range(T // BANK):
                         one_pass(b, h, g)
@@ -156,68 +163,114 @@ def tile_picked_wlerp_gelu_lo_kernel(tc, x_words, x_scales, w1, frac, left, righ
                 f_part = f_rest[:, v0 - first : v0 - first + width]
                 g_part = g_rest[:, v0 - first : v0 - first + width]
             offs = slice(v0 // 16, (v0 + width) // 16)
-            turned = [psum.tile([P, BLOCKS, P], F32, name="turned", bufs=2) for s in range(width // P)]
+            last = v0 + width == T
+            turned = [psum.tile([P, BLOCKS, P], F32, name="turned", tag="turned%d" % s, bufs=1) for s in range(width // P)]
+            dealt = [ring.tile([P, PACK, P], F32, name="dealt", bufs=6) for s in range(width // P)]
+            if last:
+                all_left = keep.tile([P, BLOCKS, width], F32, name="all_left", tag="left0", align_bytes=64)
+                all_right = keep.tile([P, BLOCKS, width], F32, name="all_right", tag="right0", align_bytes=64)
+
+            def deal(s, bank, b0, b1):
+                nc.scalar.copy(
+                    out=dealt[s][:].rearrange("p t (b l) -> p b l t", b=BLOCKS)[:, b0:b1],
+                    in_=bank[:, b0:b1, :].rearrange("p b (l t) -> p b l t", t=PACK),
+                )
+
             for b in range(BLOCKS):
-                from_left = keep.tile([P, width], F32, name="from_left", tag="left%d" % (b % 2))
-                from_right = keep.tile([P, width], F32, name="from_right", tag="right%d" % (b % 2), align_bytes=64)
-                nc.vector.tensor_tensor(from_left[:], y[b][:].indirect(left_sb[:, offs]), g_part, ALU.mult)
-                nc.vector.tensor_tensor(from_right[:], y[b][:].indirect(right_sb[:, offs]), f_part, ALU.mult)
-                for s in range(width // P):
-                    cols = slice(s * P, (s + 1) * P)
-                    nc.tensor.matmul(turned[s][:, b, :], from_left[:, cols], ident[:], start=True, stop=False, is_transpose=True)
-                    nc.tensor.matmul(turned[s][:, b, :], from_right[:, cols], ident[:], start=False, stop=True, is_transpose=True)
+                if last:
+                    from_left = all_left[:, b, :]
+                    from_right = all_right[:, b, :]
+                else:
+                    left_tile = keep.tile([P, width], F32, name="left_tile", tag="left%d" % (b % 2), align_bytes=64)
+                    right_tile = keep.tile([P, width], F32, name="right_tile", tag="right%d" % (b % 2), align_bytes=64)
+                    from_left = left_tile[:]
+                    from_right = right_tile[:]
+                nc.vector.tensor_tensor(from_left, y[b][:].indirect(left_sb[:, offs]), g_part, ALU.mult)
+                nc.vector.tensor_tensor(from_right, y[b][:].indirect(right_sb[:, offs]), f_part, ALU.mult)
+                if last and b == BLOCKS - 1:
+                    deal(0, turned[0], 0, b)
+                    turned[0] = psum.tile([P, BLOCKS, P], F32, name="turned", tag="turned1", bufs=1)
+                for source, opens in ((from_left, True), (from_right, False)):
+                    for s in range(width // P):
+                        nc.tensor.matmul(
+                            turned[s][:, b, :], source[:, s * P : (s + 1) * P], ident[:],
+                            start=opens, stop=not opens, is_transpose=True,
+                        )
                 if b == 0:
                     between()
-            dealt = []
-            for s in range(width // P):
-                tile = ring.tile([P, PACK, P], F32, name="dealt")
-                nc.scalar.copy(
-                    out=tile[:].rearrange("p t (b l) -> p t b l", b=BLOCKS),
-                    in_=turned[s][:].rearrange("p b (l t) -> p t b l", t=PACK),
+            if last:
+                deal(0, turned[0], BLOCKS - 1, BLOCKS)
+                summed = keep.tile([P, BLOCKS, width], F32, name="summed")
+                nc.vector.tensor_tensor(summed[:], all_left[:], all_right[:], ALU.add)
+                nc.sync.dma_start(
+                    out=out_0.rearrange("(b p) v -> p b v", p=P)[:, :, v0 : v0 + width], in_=summed[:]
                 )
-                dealt.append(tile)
+            else:
+                for s in range(width // P):
+                    deal(s, turned[s], 0, BLOCKS)
             return dealt
 
-        def back(v0, width, dealt, last):
-            result = ring.tile([P, PACK, width], F32, name="result")
-            rounded = ring.tile([P, width, PACK], BF16, name="rounded", align_bytes=64)
+        quant_starts = [sum(QUANT[:i]) for i in range(len(QUANT))]
+        rounded = [keep.tile([P, w, PACK], BF16, name="rounded%d" % i, align_bytes=64) for i, w in enumerate(QUANT)]
+
+        def planes(i):
+            cols = slice(quant_starts[i], quant_starts[i] + QUANT[i])
+            nc.vector.quantize_mx(
+                out=codes[:, cols].bitcast(FP8X4),
+                scales=scales[:, cols],
+                in_=rounded[i][:].rearrange("p v t -> p (v t)"),
+            )
+
+        def store_words(v0, v1):
+            nc.sync.dma_start(out=out_words[:, v0:v1], in_=codes[:, v0:v1].bitcast(I32))
+
+        held = []
+
+        def back(v0, width, dealt):
+            last = v0 + width == T
+            kept = min(width, T - 2 * P - v0)
+            if not last:
+                result = ring.tile([P, PACK, kept], F32, name="result")
             for s in range(width // P):
                 cols = slice(s * P, (s + 1) * P)
+                v = v0 + s * P
+                i = max(n for n in range(len(QUANT)) if quant_starts[n] <= v)
+                into = rounded[i][:, v - quant_starts[i] : v - quant_starts[i] + P, :]
                 bank = psum.tile([P, PACK, P], F32, name="upright", tag="bank")
                 for t in range(PACK):
                     nc.tensor.transpose(bank[:, t, :], dealt[s][:, t, :], ident[:])
-                if last:
-                    nc.vector.tensor_copy(out=rounded[:, cols, :], in_=bank[:].rearrange("p t v -> p v t"))
+                if v >= T - 2 * P:
+                    nc.vector.tensor_copy(out=into, in_=bank[:].rearrange("p t v -> p v t"))
+                if v == T - 2 * P:
+                    held.append((v, bank))
+                elif not last:
                     nc.scalar.copy(out=result[:, :, cols], in_=bank[:])
-                else:
-                    nc.scalar.copy(out=result[:, :, cols], in_=bank[:])
-                    nc.scalar.copy(out=rounded[:, cols, :], in_=bank[:].rearrange("p t v -> p v t"))
-            nc.sync.dma_start(out=out_rows[:, :, v0 : v0 + width], in_=result[:])
-            return rounded
-
-        def planes(v0, width, rounded):
-            nc.vector.quantize_mx(
-                out=codes[:, v0 : v0 + width].bitcast(FP8X4),
-                scales=scales[:, v0 : v0 + width],
-                in_=rounded[:].rearrange("p v t -> p (v t)"),
-            )
-            nc.sync.dma_start(out=out_words[:, v0 : v0 + width], in_=codes[:, v0 : v0 + width].bitcast(I32))
+                if v < T - 2 * P:
+                    nc.scalar.copy(out=into, in_=bank[:].rearrange("p t v -> p v t"))
+            if not last:
+                nc.sync.dma_start(out=out_rows[:, :, v0 : v0 + kept], in_=result[:])
 
         starts = [sum(CHUNKS[:c]) for c in range(len(CHUNKS))]
         dealt_of = {}
-        rounded_of = {}
 
         def finish(c):
             if c >= 0:
-                rounded_of[c] = back(starts[c], CHUNKS[c], dealt_of[c], c == len(CHUNKS) - 1)
+                back(starts[c], CHUNKS[c], dealt_of[c])
 
         for c in range(len(CHUNKS)):
             dealt_of[c] = front(starts[c], CHUNKS[c], lambda: finish(c - 1))
-            if c >= 1:
-                planes(starts[c - 1], CHUNKS[c - 1], rounded_of[c - 1])
-        last = len(CHUNKS) - 1
-        finish(last)
-        planes(starts[last], CHUNKS[last], rounded_of[last])
+            if c == 2:
+                planes(0)
+                store_words(0, quant_starts[1])
+        late = ring.tile([P, PACK, P], F32, name="result")
+        nc.scalar.copy(out=late[:], in_=held[0][1][:])
+        nc.sync.dma_start(out=out_rows[:, :, held[0][0] : held[0][0] + P], in_=late[:])
+        planes(1)
+        planes(2)
+        store_words(quant_starts[1], quant_starts[3])
+        finish(len(CHUNKS) - 1)
+        planes(3)
+        store_words(quant_starts[3], T)
 
         for q in range(4):
             queue = nc.sync if q % 2 == 0 else nc.scalar

from contextlib import ExitStack

import concourse.mybir as mybir
from concourse.masks import make_identity

K, T, N = 1024, 1024, 512
FLOPS = 2 * K * T * N

F32 = mybir.dt.float32
BF16 = mybir.dt.bfloat16
I32 = mybir.dt.int32
U32 = mybir.dt.uint32
U16 = mybir.dt.uint16
U8 = mybir.dt.uint8
FP8X4 = mybir.dt.float8_e4m3fn_x4
FP4X4 = mybir.dt.float4_e2m1fn_x4
ALU = mybir.AluOpType
ACT = mybir.ActivationFunctionType

P = 128
PACK = 4
PASSES = K // (P * PACK)
BANK = 512
BLOCKS = N // P
CHUNKS = (384, 256, 256, 128)
QUANT = (512, 256, 128, 128)


def tile_picked_wlerp_gelu_lo_kernel(tc, x_words, x_scales, w1, frac, left, right, out_0, out_1, out_2):
    nc = tc.nc
    with ExitStack() as ctx:
        keep = ctx.enter_context(tc.tile_pool(name="keep", bufs=1))
        ring = ctx.enter_context(tc.tile_pool(name="ring", bufs=4))
        psum = ctx.enter_context(tc.psum_pool(name="psum", bufs=5))

        left_sb = keep.tile([P, T // 16], U16, name="left_sb")
        right_sb = keep.tile([P, T // 16], U16, name="right_sb")

        xs = keep.tile([P, PASSES, T], U8, name="xs", align_bytes=64)
        nc.gpsimd.memset(xs[:].rearrange("p g c -> p (g c)").bitcast(I32), 0)
        warm_in = keep.tile([P, 1], F32, name="warm_in")
        warm_out = keep.tile([P, 1], F32, name="warm_out")
        nc.gpsimd.memset(warm_in[:], 0.0)
        nc.scalar.activation(out=warm_out[:], in_=warm_in[:], func=ACT.Gelu_apprx_tanh)

        ident = keep.tile([P, P], F32, name="ident")
        make_identity(nc, ident[:])

        raw = {}
        xw = {}

        def load_w(b, g, blocks):
            label = "raw%d%d" % (b, g)
            tile = keep.tile([P, PACK, blocks * P], F32, name=label)
            rows = w1[g * P * PACK : (g + 1) * P * PACK, b * P : (b + blocks) * P]
            nc.sync.dma_start(out=tile[:], in_=rows.rearrange("(p j) c -> p j c", j=PACK))
            for i in range(blocks):
                raw[b + i, g] = tile[:, :, i * P : (i + 1) * P]

        def load_x(g):
            xw[g] = keep.tile([P, 2 * T], U8, name="xw%d" % g, align_bytes=64)
            nc.sync.dma_start(out=xw[g][:].bitcast(I32), in_=x_words[g].bitcast(I32))

        first = CHUNKS[0]
        f_head = keep.tile([P, first], F32, name="f_head")
        g_head = keep.tile([P, first], F32, name="g_head")
        f_rest = keep.tile([P, T - first], F32, name="f_rest")
        g_rest = keep.tile([P, T - first], F32, name="g_rest")

        load_w(0, 0, 2)
        load_x(0)
        for q in range(4):
            nc.sync.dma_start(
                out=xs[32 * q : 32 * q + 4, :, :].bitcast(I32),
                in_=x_scales[:, 4 * q : 4 * q + 4, :].rearrange("g r c -> r g c").bitcast(I32),
            )
        load_w(0, 1, 2)
        load_x(1)
        nc.sync.dma_start(out=f_head[:], in_=frac[:, 0:first])
        nc.sync.dma_start(left_sb[:], left)
        nc.sync.dma_start(right_sb[:], right)
        for b in (2, 3):
            for g in range(PASSES):
                load_w(b, g, 1)
        nc.sync.dma_start(out=f_rest[:], in_=frac[:, first:T])

        w_codes = {}
        w_scales = {}

        grouped_tag = {(0, 1): "hold", (2, 0): "left0", (2, 1): "right0", (3, 0): "right1", (3, 1): "left1"}
        codes_tag = {(1, 0): "hold"}

        def quantize_w(b, g):
            label = "%d%d" % (b, g)
            grouped = keep.tile(
                [P, P, PACK], BF16, name="wg" + label, tag=grouped_tag.get((b, g), "wg" + label), align_bytes=64
            )
            dst = grouped[:].rearrange("p (c i) j -> p c j i", i=4)
            src = raw[b, g].rearrange("p j (c i) -> p c j i", i=4)
            if (b, g) == (3, 0):
                nc.scalar.copy(out=dst, in_=src)
            else:
                nc.vector.tensor_copy(out=dst, in_=src)
            wc = keep.tile([P, P], U32, name="wc" + label, tag=codes_tag.get((b, g), "wc" + label), align_bytes=64)
            ws = keep.tile([P, P], U8, name="ws" + label, align_bytes=64)
            nc.vector.quantize_mx(
                out=wc[:].bitcast(FP8X4),
                scales=ws[:],
                in_=grouped[:].rearrange("p c j -> p (c j)"),
            )
            w_codes[b, g] = wc[:]
            w_scales[b, g] = ws[:]

        y = [keep.tile([P, T], F32, name="y%d" % b) for b in range(BLOCKS)]

        def project(a):
            blocks = (2 * a, 2 * a + 1)
            acc = {}
            for b in blocks:
                for h in range(T // BANK):
                    acc[b, h] = psum.tile([P, BANK], F32, name="acc%d%d" % (b, h), tag="bank")

            def one_pass(b, h, g):
                nc.tensor.matmul_mx(
                    out=acc[b, h][:],
                    lhsT=w_codes[b, g].bitcast(FP8X4),
                    lhsT_scale=w_scales[b, g],
                    rhs=xw[g][:, 2 * h * BANK : 2 * (h + 1) * BANK].bitcast(FP4X4),
                    rhs_scale=xs[:, g, h * BANK : (h + 1) * BANK],
                    start=(g == 0),
                    stop=(g == PASSES - 1),
                )

            for b in blocks:
                quantize_w(b, 0)
                quantize_w(b, 1)
                for g in range(PASSES):
                    for h in range(T // BANK):
                        one_pass(b, h, g)
                        if g == PASSES - 1:
                            nc.scalar.activation(
                                out=y[b][:, h * BANK : (h + 1) * BANK],
                                in_=acc[b, h][:],
                                func=ACT.Gelu_apprx_tanh,
                            )

        project(0)
        nc.vector.tensor_scalar(
            out=g_head[:], in0=f_head[:], scalar1=-1.0, scalar2=1.0, op0=ALU.mult, op1=ALU.add
        )
        project(1)
        nc.scalar.activation(out=g_rest[:], in_=f_rest[:], func=ACT.Copy, scale=-1.0, bias=1.0)

        codes = keep.tile([P, T], U32, name="codes", align_bytes=64)
        scales = keep.tile([P, T], U8, name="scales", align_bytes=64)
        out_rows = out_0.rearrange("(l t) v -> l t v", t=PACK)
        out_words = out_1[0].rearrange("l v t -> l (v t)").bitcast(I32)

        def front(v0, width, between):
            if v0 == 0:
                f_part, g_part = f_head[:], g_head[:]
            else:
                f_part = f_rest[:, v0 - first : v0 - first + width]
                g_part = g_rest[:, v0 - first : v0 - first + width]
            offs = slice(v0 // 16, (v0 + width) // 16)
            last = v0 + width == T
            turned = [psum.tile([P, BLOCKS, P], F32, name="turned", tag="turned%d" % s, bufs=1) for s in range(width // P)]
            dealt = [ring.tile([P, PACK, P], F32, name="dealt", bufs=6) for s in range(width // P)]
            if last:
                all_left = keep.tile([P, BLOCKS, width], F32, name="all_left", tag="left0", align_bytes=64)
                all_right = keep.tile([P, BLOCKS, width], F32, name="all_right", tag="right0", align_bytes=64)

            def deal(s, bank, b0, b1):
                nc.scalar.copy(
                    out=dealt[s][:].rearrange("p t (b l) -> p b l t", b=BLOCKS)[:, b0:b1],
                    in_=bank[:, b0:b1, :].rearrange("p b (l t) -> p b l t", t=PACK),
                )

            for b in range(BLOCKS):
                if last:
                    from_left = all_left[:, b, :]
                    from_right = all_right[:, b, :]
                else:
                    left_tile = keep.tile([P, width], F32, name="left_tile", tag="left%d" % (b % 2), align_bytes=64)
                    right_tile = keep.tile([P, width], F32, name="right_tile", tag="right%d" % (b % 2), align_bytes=64)
                    from_left = left_tile[:]
                    from_right = right_tile[:]
                nc.vector.tensor_tensor(from_left, y[b][:].indirect(left_sb[:, offs]), g_part, ALU.mult)
                nc.vector.tensor_tensor(from_right, y[b][:].indirect(right_sb[:, offs]), f_part, ALU.mult)
                if last and b == BLOCKS - 1:
                    deal(0, turned[0], 0, b)
                    turned[0] = psum.tile([P, BLOCKS, P], F32, name="turned", tag="turned1", bufs=1)
                for source, opens in ((from_left, True), (from_right, False)):
                    for s in range(width // P):
                        nc.tensor.matmul(
                            turned[s][:, b, :], source[:, s * P : (s + 1) * P], ident[:],
                            start=opens, stop=not opens, is_transpose=True,
                        )
                if b == 0:
                    between()
            if last:
                deal(0, turned[0], BLOCKS - 1, BLOCKS)
                summed = keep.tile([P, BLOCKS, width], F32, name="summed")
                nc.vector.tensor_tensor(summed[:], all_left[:], all_right[:], ALU.add)
                nc.sync.dma_start(
                    out=out_0.rearrange("(b p) v -> p b v", p=P)[:, :, v0 : v0 + width], in_=summed[:]
                )
            else:
                for s in range(width // P):
                    deal(s, turned[s], 0, BLOCKS)
            return dealt

        quant_starts = [sum(QUANT[:i]) for i in range(len(QUANT))]
        rounded = [keep.tile([P, w, PACK], BF16, name="rounded%d" % i, align_bytes=64) for i, w in enumerate(QUANT)]

        def planes(i):
            cols = slice(quant_starts[i], quant_starts[i] + QUANT[i])
            nc.vector.quantize_mx(
                out=codes[:, cols].bitcast(FP8X4),
                scales=scales[:, cols],
                in_=rounded[i][:].rearrange("p v t -> p (v t)"),
            )

        def store_words(v0, v1):
            nc.sync.dma_start(out=out_words[:, v0:v1], in_=codes[:, v0:v1].bitcast(I32))

        held = []

        def back(v0, width, dealt):
            last = v0 + width == T
            kept = min(width, T - 2 * P - v0)
            if not last:
                result = ring.tile([P, PACK, kept], F32, name="result")
            for s in range(width // P):
                cols = slice(s * P, (s + 1) * P)
                v = v0 + s * P
                i = max(n for n in range(len(QUANT)) if quant_starts[n] <= v)
                into = rounded[i][:, v - quant_starts[i] : v - quant_starts[i] + P, :]
                bank = psum.tile([P, PACK, P], F32, name="upright", tag="bank")
                for t in range(PACK):
                    nc.tensor.transpose(bank[:, t, :], dealt[s][:, t, :], ident[:])
                if v >= T - 2 * P:
                    nc.vector.tensor_copy(out=into, in_=bank[:].rearrange("p t v -> p v t"))
                if v == T - 2 * P:
                    held.append((v, bank))
                elif not last:
                    nc.scalar.copy(out=result[:, :, cols], in_=bank[:])
                if v < T - 2 * P:
                    nc.scalar.copy(out=into, in_=bank[:].rearrange("p t v -> p v t"))
            if not last:
                nc.sync.dma_start(out=out_rows[:, :, v0 : v0 + kept], in_=result[:])

        starts = [sum(CHUNKS[:c]) for c in range(len(CHUNKS))]
        dealt_of = {}

        def finish(c):
            if c >= 0:
                back(starts[c], CHUNKS[c], dealt_of[c])

        for c in range(len(CHUNKS)):
            dealt_of[c] = front(starts[c], CHUNKS[c], lambda: finish(c - 1))
            if c == 2:
                planes(0)
                store_words(0, quant_starts[1])
        late = ring.tile([P, PACK, P], F32, name="result")
        nc.scalar.copy(out=late[:], in_=held[0][1][:])
        nc.sync.dma_start(out=out_rows[:, :, held[0][0] : held[0][0] + P], in_=late[:])
        planes(1)
        planes(2)
        store_words(quant_starts[1], quant_starts[3])
        finish(len(CHUNKS) - 1)
        planes(3)
        store_words(quant_starts[3], T)

        for q in range(4):
            queue = nc.sync if q % 2 == 0 else nc.scalar
            queue.dma_start(
                out=out_2[0, 4 * q : 4 * q + 4, :].bitcast(I32),
                in_=scales[32 * q : 32 * q + 4, :].bitcast(I32),
            )
